import numpy as np
import ml_dtypes


def mxq(x, axis, fmt="e4m3"):
    dtype, down = {"e4m3": (ml_dtypes.float8_e4m3fn, 7), "e5m2": (ml_dtypes.float8_e5m2, 14)}[fmt]
    v = np.moveaxis(np.asarray(x, np.float32).astype(ml_dtypes.bfloat16).astype(np.float64), axis, -1)
    blocks = v.reshape(v.shape[:-1] + (-1, 32))
    amax = np.abs(blocks).max(-1, keepdims=True)
    byte = np.maximum(np.where(amax > 0, np.frexp(amax)[1] - 1 + 127, 0) - down, 1)
    scale = np.exp2(byte - 127.0)
    codes = (blocks / scale).astype(np.float32).astype(dtype).astype(np.float64)
    return np.moveaxis((codes * scale).reshape(v.shape), -1, axis)


WIDE = False


def mx_kscale(k):
    if not WIDE:
        return np.ones(k)
    levels = np.array([10, -10, 5, -5, 0])
    if k % 512:
        return np.exp2(np.random.permutation(np.resize(levels, k // 32))).repeat(32)
    a = np.empty((k // 512, 16))
    for p in range(k // 512):
        a[p, :8] = np.random.permutation(np.resize(levels, 8))
        for g in range(8):
            far = levels[np.abs(levels - a[p, g]) >= 10]
            a[p, g + 8] = far[np.random.randint(len(far))]
    return np.exp2(a.ravel()).repeat(32)


def f64(x):
    return np.asarray(x).astype(np.float64)


def striped(idx):
    return np.tile(idx.reshape(-1, 16).T, (8, 1)).astype(np.uint16)


def unstriped(offs):
    return offs[:16].T.reshape(-1).astype(np.int64)


K, T, D, S, V, N = 512, 2048, 2, 1536, 768, 256


def setup_inputs():
    n = np.random.standard_normal
    s = mx_kscale(K)[:, None]
    return {
        "xT": (n((K, T)) * s).astype(np.float32),
        "w": (n((D, K, N)) / np.sqrt(D * K) / s[None]).astype(np.float32),
        "b": (0.3 * n((N, 1))).astype(np.float32),
        "gate": np.tile(np.random.uniform(0.2, 1.0, S), (N, 1)).astype(np.float32),
        "offs": striped(np.random.permutation(T)[:S]),
    }


def reference(xT, w, b, gate, offs):
    idx = unstriped(offs)
    xq = mxq(f64(xT)[:, idx], 0, "e4m3")
    wq = mxq(f64(w), 1, "e4m3")
    y = sum(wq[d].T @ xq[:, d * V:(d + 1) * V] for d in range(D))
    y = y + f64(b)
    out = np.zeros((N, T))
    out[:, idx] = f64(gate) * np.tile(y, (1, D))
    return out

@@ -1,0 +1,144 @@
+from contextlib import ExitStack
+
+import concourse.mybir as mybir
+
+K, T, D, S, V, N = 512, 2048, 2, 1536, 768, 256
+FLOPS = 2 * K * D * V * N
+
+F32 = mybir.dt.float32
+BF16 = mybir.dt.bfloat16
+U32 = mybir.dt.uint32
+U16 = mybir.dt.uint16
+U8 = mybir.dt.uint8
+FP8X4 = mybir.dt.float8_e4m3fn_x4
+COPY = mybir.ActivationFunctionType.Copy
+MULT = mybir.AluOpType.mult
+ADD = mybir.AluOpType.add
+
+P = 128
+PACK = 4
+MB = N // P
+C = 256
+CHUNKS = V // C
+HALF = T // 2
+
+
+def tile_picked_tome_lin_bias_sub_e_kernel(tc, xT, w, b, gate, offs, out):
+    nc = tc.nc
+    with ExitStack() as ctx:
+        keep = ctx.enter_context(tc.tile_pool(name="keep", bufs=1))
+        psum = ctx.enter_context(tc.psum_pool(name="psum", bufs=1))
+
+        lists = keep.tile([P, S // 16], U16, name="lists")
+        nc.sync.dma_start(lists[:], offs)
+
+        x_rows = xT.rearrange("(p j) t -> p j t", j=PACK)
+        x32 = [keep.tile([P, T], F32, name=f"x32_{j}") for j in range(PACK)]
+        x16 = [keep.tile([P, T], BF16, name=f"x16_{j}") for j in range(PACK)]
+        for j in range(PACK):
+            for h in range(2):
+                cols = slice(h * HALF, (h + 1) * HALF)
+                nc.sync.dma_start(x32[j][:, cols], x_rows[:, j, cols])
+
+        w32 = [keep.tile([P, PACK, N], F32, name=f"w32_{d}") for d in range(D)]
+        for d in range(D):
+            nc.sync.dma_start(w32[d][:], w[d].rearrange("(p j) n -> p j n", j=PACK))
+        bias = [keep.tile([P, 1], F32, name=f"bias_{m}") for m in range(MB)]
+        for m in range(MB):
+            nc.sync.dma_start(bias[m][:], b[m * P : (m + 1) * P, :])
+        gates = [keep.tile([P, MB, V], F32, name=f"gate_{d}") for d in range(D)]
+        gate_rows = gate.rearrange("(m p) s -> p m s", p=P)
+        for d in range(D):
+            nc.sync.dma_start(gates[d][:], gate_rows[:, :, d * V : (d + 1) * V])
+
+        window = [keep.tile([P, T], F32, name=f"window_{m}") for m in range(MB)]
+        for m in range(MB):
+            nc.gpsimd.memset(window[m][:], 0.0)
+
+        def entries(c, d):
+            first = (d * V + c * C) // 16
+            return lists[:, first : first + C // 16]
+
+        grouped = [keep.tile([P, D * C, PACK], BF16, name=f"grouped_{c}", align_bytes=64) for c in range(CHUNKS)]
+        x_codes = [keep.tile([P, D * C], U32, name=f"x_codes_{c}", align_bytes=64) for c in range(CHUNKS)]
+        x_scales = [keep.tile([P, D * C], U8, name=f"x_scales_{c}", align_bytes=64) for c in range(CHUNKS)]
+        w16 = [keep.tile([P, N, PACK], BF16, name=f"w16_{d}", align_bytes=64) for d in range(D)]
+        w_codes = [keep.tile([P, N], U32, name=f"w_codes_{d}", align_bytes=64) for d in range(D)]
+        w_scales = [keep.tile([P, N], U8, name=f"w_scales_{d}", align_bytes=64) for d in range(D)]
+        z = [
+            [[keep.tile([P, C], F32, name=f"z_{c}_{d}_{m}") for m in range(MB)] for d in range(D)] for c in range(CHUNKS)
+        ]
+        banks = [[psum.tile([P, C], F32, name=f"bank_{c}_{m}") for m in range(MB)] for c in range(CHUNKS)]
+
+        for j in range(PACK):
+            for h in range(2):
+                cols = slice(h * HALF, (h + 1) * HALF)
+                nc.scalar.activation(x16[j][:, cols], x32[j][:, cols], COPY)
+            for d in range(D):
+                nc.vector.tensor_copy(grouped[0][:, d * C : (d + 1) * C, j], x32[j][:].indirect(entries(0, d)))
+
+        def quantize_x(c):
+            nc.vector.quantize_mx(
+                out=x_codes[c][:].bitcast(FP8X4),
+                scales=x_scales[c][:],
+                in_=grouped[c][:].rearrange("p n j -> p (n j)"),
+            )
+
+        def multiply(c):
+            for m in range(MB):
+                rows = slice(m * P, (m + 1) * P)
+                for d in range(D):
+                    cols = slice(d * C, (d + 1) * C)
+                    nc.tensor.matmul_mx(
+                        out=banks[c][m][:],
+                        lhsT=w_codes[d][:, rows].bitcast(FP8X4),
+                        lhsT_scale=w_scales[d][:, rows],
+                        rhs=x_codes[c][:, cols].bitcast(FP8X4),
+                        rhs_scale=x_scales[c][:, cols],
+                        start=(d == 0),
+                        stop=(d == D - 1),
+                    )
+
+        def weigh(c, d):
+            for m in range(MB):
+                nc.vector.scalar_tensor_tensor(
+                    z[c][d][m][:], banks[c][m][:], bias[m][:], gates[d][:, m, c * C : (c + 1) * C], ADD, MULT
+                )
+
+        def scatter(c, d):
+            for m in range(MB):
+                nc.vector.tensor_copy(window[m][:].indirect(entries(c, d)), z[c][d][m][:])
+
+        def gather_scalar(c):
+            for j in range(PACK):
+                for d in range(D):
+                    nc.scalar.activation(
+                        grouped[c][:, d * C : (d + 1) * C, j], x16[j][:].indirect(entries(c, d)), COPY
+                    )
+
+        for d in range(D):
+            nc.vector.tensor_copy(w16[d][:], w32[d][:].rearrange("p j n -> p n j"))
+        quantize_x(0)
+        for d in range(D):
+            nc.vector.quantize_mx(
+                out=w_codes[d][:].bitcast(FP8X4),
+                scales=w_scales[d][:],
+                in_=w16[d][:].rearrange("p n j -> p (n j)"),
+            )
+        multiply(0)
+        weigh(0, 0)
+        weigh(0, 1)
+        gather_scalar(1)
+        for c in range(1, CHUNKS):
+            scatter(c - 1, 0)
+            quantize_x(c)
+            multiply(c)
+            scatter(c - 1, 1)
+            weigh(c, 0)
+            weigh(c, 1)
+            if c + 1 < CHUNKS:
+                gather_scalar(c + 1)
+        scatter(CHUNKS - 1, 0)
+        scatter(CHUNKS - 1, 1)
+        for m in range(MB):
+            nc.sync.dma_start(out[m * P : (m + 1) * P, :], window[m][:])

@@ -12,6 +12,7 @@ U16 = mybir.dt.uint16
 U8 = mybir.dt.uint8
 FP8X4 = mybir.dt.float8_e4m3fn_x4
 COPY = mybir.ActivationFunctionType.Copy
+IDENT = mybir.ActivationFunctionType.Identity
 MULT = mybir.AluOpType.mult
 ADD = mybir.AluOpType.add
 
@@ -32,6 +33,9 @@ def tile_picked_tome_lin_bias_sub_e_kernel(tc, xT, w, b, gate, offs, out):
         lists = keep.tile([P, S // 16], U16, name="lists")
         nc.sync.dma_start(lists[:], offs)
 
+        bias = [keep.tile([P, 1], F32, name=f"bias_{m}") for m in range(MB)]
+        for m in range(MB):
+            nc.scalar.dma_start(bias[m][:], b[m * P : (m + 1) * P, :])
         x_rows = xT.rearrange("(p j) t -> p j t", j=PACK)
         x32 = [keep.tile([P, T], F32, name=f"x32_{j}") for j in range(PACK)]
         x16 = [keep.tile([P, T], BF16, name=f"x16_{j}") for j in range(PACK)]
@@ -43,13 +47,11 @@ def tile_picked_tome_lin_bias_sub_e_kernel(tc, xT, w, b, gate, offs, out):
         w32 = [keep.tile([P, PACK, N], F32, name=f"w32_{d}") for d in range(D)]
         for d in range(D):
             nc.sync.dma_start(w32[d][:], w[d].rearrange("(p j) n -> p j n", j=PACK))
-        bias = [keep.tile([P, 1], F32, name=f"bias_{m}") for m in range(MB)]
-        for m in range(MB):
-            nc.sync.dma_start(bias[m][:], b[m * P : (m + 1) * P, :])
-        gates = [keep.tile([P, MB, V], F32, name=f"gate_{d}") for d in range(D)]
-        gate_rows = gate.rearrange("(m p) s -> p m s", p=P)
-        for d in range(D):
-            nc.sync.dma_start(gates[d][:], gate_rows[:, :, d * V : (d + 1) * V])
+        gates = [[keep.tile([P, D, C], F32, name=f"gate_{c}_{m}") for m in range(MB)] for c in range(CHUNKS)]
+        for c in range(CHUNKS):
+            for m in range(MB):
+                rows = gate[m * P : (m + 1) * P, :].rearrange("p (d v) -> p d v", d=D)
+                nc.sync.dma_start(gates[c][m][:], rows[:, :, c * C : (c + 1) * C])
 
         window = [keep.tile([P, T], F32, name=f"window_{m}") for m in range(MB)]
         for m in range(MB):
@@ -59,15 +61,18 @@ def tile_picked_tome_lin_bias_sub_e_kernel(tc, xT, w, b, gate, offs, out):
             first = (d * V + c * C) // 16
             return lists[:, first : first + C // 16]
 
-        grouped = [keep.tile([P, D * C, PACK], BF16, name=f"grouped_{c}", align_bytes=64) for c in range(CHUNKS)]
-        x_codes = [keep.tile([P, D * C], U32, name=f"x_codes_{c}", align_bytes=64) for c in range(CHUNKS)]
-        x_scales = [keep.tile([P, D * C], U8, name=f"x_scales_{c}", align_bytes=64) for c in range(CHUNKS)]
+        def chunk_tiles(c):
+            grouped = keep.tile([P, D * C, PACK], BF16, name="grouped", tag="by_vector" if c == 0 else "by_scalar", align_bytes=64)
+            codes = keep.tile([P, D * C], U32, name="x_codes", tag="x_codes", align_bytes=64)
+            scales = keep.tile([P, D * C], U8, name="x_scales", tag="x_scales", align_bytes=64)
+            return grouped, codes, scales
+
+        tiles = {0: chunk_tiles(0)}
+        grouped = tiles[0][0]
         w16 = [keep.tile([P, N, PACK], BF16, name=f"w16_{d}", align_bytes=64) for d in range(D)]
         w_codes = [keep.tile([P, N], U32, name=f"w_codes_{d}", align_bytes=64) for d in range(D)]
         w_scales = [keep.tile([P, N], U8, name=f"w_scales_{d}", align_bytes=64) for d in range(D)]
-        z = [
-            [[keep.tile([P, C], F32, name=f"z_{c}_{d}_{m}") for m in range(MB)] for d in range(D)] for c in range(CHUNKS)
-        ]
+        y = [[keep.tile([P, C], F32, name=f"y_{c}_{m}") for m in range(MB)] for c in range(CHUNKS)]
         banks = [[psum.tile([P, C], F32, name=f"bank_{c}_{m}") for m in range(MB)] for c in range(CHUNKS)]
 
         for j in range(PACK):
@@ -75,16 +80,16 @@ def tile_picked_tome_lin_bias_sub_e_kernel(tc, xT, w, b, gate, offs, out):
                 cols = slice(h * HALF, (h + 1) * HALF)
                 nc.scalar.activation(x16[j][:, cols], x32[j][:, cols], COPY)
             for d in range(D):
-                nc.vector.tensor_copy(grouped[0][:, d * C : (d + 1) * C, j], x32[j][:].indirect(entries(0, d)))
+                nc.vector.tensor_copy(grouped[:, d * C : (d + 1) * C, j], x32[j][:].indirect(entries(0, d)))
 
         def quantize_x(c):
+            grouped, codes, scales = tiles[c]
             nc.vector.quantize_mx(
-                out=x_codes[c][:].bitcast(FP8X4),
-                scales=x_scales[c][:],
-                in_=grouped[c][:].rearrange("p n j -> p (n j)"),
+                out=codes[:].bitcast(FP8X4), scales=scales[:], in_=grouped[:].rearrange("p n j -> p (n j)")
             )
 
         def multiply(c):
+            grouped, codes, scales = tiles[c]
             for m in range(MB):
                 rows = slice(m * P, (m + 1) * P)
                 for d in range(D):
@@ -93,52 +98,67 @@ def tile_picked_tome_lin_bias_sub_e_kernel(tc, xT, w, b, gate, offs, out):
                         out=banks[c][m][:],
                         lhsT=w_codes[d][:, rows].bitcast(FP8X4),
                         lhsT_scale=w_scales[d][:, rows],
-                        rhs=x_codes[c][:, cols].bitcast(FP8X4),
-                        rhs_scale=x_scales[c][:, cols],
+                        rhs=codes[:, cols].bitcast(FP8X4),
+                        rhs_scale=scales[:, cols],
                         start=(d == 0),
                         stop=(d == D - 1),
                     )
 
-        def weigh(c, d):
-            for m in range(MB):
-                nc.vector.scalar_tensor_tensor(
-                    z[c][d][m][:], banks[c][m][:], bias[m][:], gates[d][:, m, c * C : (c + 1) * C], ADD, MULT
-                )
-
-        def scatter(c, d):
-            for m in range(MB):
-                nc.vector.tensor_copy(window[m][:].indirect(entries(c, d)), z[c][d][m][:])
+        def scatter(c, d, m):
+            nc.vector.tensor_tensor(
+                window[m][:].indirect(entries(c, d)), y[c][m][:], gates[c][m][:, d, :], MULT
+            )
 
         def gather_scalar(c):
+            tiles[c] = chunk_tiles(c)
+            grouped = tiles[c][0]
             for j in range(PACK):
                 for d in range(D):
                     nc.scalar.activation(
-                        grouped[c][:, d * C : (d + 1) * C, j], x16[j][:].indirect(entries(c, d)), COPY
+                        grouped[:, d * C : (d + 1) * C, j], x16[j][:].indirect(entries(c, d)), COPY
                     )
 
-        for d in range(D):
+        def cast_w(d):
             nc.vector.tensor_copy(w16[d][:], w32[d][:].rearrange("p j n -> p n j"))
-        quantize_x(0)
-        for d in range(D):
+
+        def quantize_w(d):
             nc.vector.quantize_mx(
                 out=w_codes[d][:].bitcast(FP8X4),
                 scales=w_scales[d][:],
                 in_=w16[d][:].rearrange("p n j -> p (n j)"),
             )
+
+        def leave_bank(c):
+            for m in range(MB):
+                nc.scalar.activation(y[c][m][:], banks[c][m][:], IDENT, bias=bias[m][:])
+
+        cast_w(0)
+        quantize_x(0)
+        cast_w(1)
+        quantize_w(0)
+        quantize_w(1)
         multiply(0)
-        weigh(0, 0)
-        weigh(0, 1)
-        gather_scalar(1)
-        for c in range(1, CHUNKS):
-            scatter(c - 1, 0)
-            quantize_x(c)
-            multiply(c)
-            scatter(c - 1, 1)
-            weigh(c, 0)
-            weigh(c, 1)
-            if c + 1 < CHUNKS:
-                gather_scalar(c + 1)
-        scatter(CHUNKS - 1, 0)
-        scatter(CHUNKS - 1, 1)
         for m in range(MB):
-            nc.sync.dma_start(out[m * P : (m + 1) * P, :], window[m][:])
+            nc.vector.tensor_scalar(y[0][m][:], banks[0][m][:], bias[m][:], None, ADD)
+        gather_scalar(1)
+        scatter(0, 0, 0)
+        scatter(0, 0, 1)
+        quantize_x(1)
+        multiply(1)
+        leave_bank(1)
+        scatter(0, 1, 0)
+        scatter(0, 1, 1)
+        gather_scalar(2)
+        scatter(1, 0, 0)
+        scatter(1, 0, 1)
+        scatter(1, 1, 0)
+        quantize_x(2)
+        multiply(2)
+        leave_bank(2)
+        scatter(1, 1, 1)
+        scatter(2, 0, 0)
+        scatter(2, 0, 1)
+        scatter(2, 1, 0)
+        nc.sync.dma_start(out[0:P, :], window[0][:])
+        scatter(2, 1, 1)
+        nc.sync.dma_start(out[P:, :], window[1][:])

@@ -44,14 +44,20 @@ def tile_picked_tome_lin_bias_sub_e_kernel(tc, xT, w, b, gate, offs, out):
                 cols = slice(h * HALF, (h + 1) * HALF)
                 nc.sync.dma_start(x32[j][:, cols], x_rows[:, j, cols])
 
-        w32 = [keep.tile([P, PACK, N], F32, name=f"w32_{d}") for d in range(D)]
-        for d in range(D):
-            nc.sync.dma_start(w32[d][:], w[d].rearrange("(p j) n -> p j n", j=PACK))
+        w32 = [keep.tile([P, D, PACK, P], F32, name=f"w32_{m}") for m in range(MB)]
         gates = [[keep.tile([P, D, C], F32, name=f"gate_{c}_{m}") for m in range(MB)] for c in range(CHUNKS)]
-        for c in range(CHUNKS):
+
+        def load_gate(c, m):
+            rows = gate[m * P : (m + 1) * P, :].rearrange("p (d v) -> p d v", d=D)
+            nc.sync.dma_start(gates[c][m][:], rows[:, :, c * C : (c + 1) * C])
+
+        for m in range(MB):
+            for d in range(D):
+                nc.sync.dma_start(w32[m][:, d], w[d].rearrange("(p j) n -> p j n", j=PACK)[:, :, m * P : (m + 1) * P])
+            load_gate(0, m)
+        for c in range(1, CHUNKS):
             for m in range(MB):
-                rows = gate[m * P : (m + 1) * P, :].rearrange("p (d v) -> p d v", d=D)
-                nc.sync.dma_start(gates[c][m][:], rows[:, :, c * C : (c + 1) * C])
+                load_gate(c, m)
 
         window = [keep.tile([P, T], F32, name=f"window_{m}") for m in range(MB)]
         for m in range(MB):
@@ -69,18 +75,21 @@ def tile_picked_tome_lin_bias_sub_e_kernel(tc, xT, w, b, gate, offs, out):
 
         tiles = {0: chunk_tiles(0)}
         grouped = tiles[0][0]
-        w16 = [keep.tile([P, N, PACK], BF16, name=f"w16_{d}", align_bytes=64) for d in range(D)]
-        w_codes = [keep.tile([P, N], U32, name=f"w_codes_{d}", align_bytes=64) for d in range(D)]
-        w_scales = [keep.tile([P, N], U8, name=f"w_scales_{d}", align_bytes=64) for d in range(D)]
+        w16 = [keep.tile([P, D, P, PACK], BF16, name=f"w16_{m}", align_bytes=64) for m in range(MB)]
+        w_codes = [keep.tile([P, D * P], U32, name=f"w_codes_{m}", align_bytes=64) for m in range(MB)]
+        w_scales = [keep.tile([P, D * P], U8, name=f"w_scales_{m}", align_bytes=64) for m in range(MB)]
         y = [[keep.tile([P, C], F32, name=f"y_{c}_{m}") for m in range(MB)] for c in range(CHUNKS)]
         banks = [[psum.tile([P, C], F32, name=f"bank_{c}_{m}") for m in range(MB)] for c in range(CHUNKS)]
 
         for j in range(PACK):
             for h in range(2):
                 cols = slice(h * HALF, (h + 1) * HALF)
-                nc.scalar.activation(x16[j][:, cols], x32[j][:, cols], COPY)
+                if h == 0 or j >= 2:
+                    nc.scalar.activation(x16[j][:, cols], x32[j][:, cols], COPY)
             for d in range(D):
                 nc.vector.tensor_copy(grouped[:, d * C : (d + 1) * C, j], x32[j][:].indirect(entries(0, d)))
+            if j < 2:
+                nc.vector.tensor_copy(x16[j][:, HALF:], x32[j][:, HALF:])
 
         def quantize_x(c):
             grouped, codes, scales = tiles[c]
@@ -88,21 +97,20 @@ def tile_picked_tome_lin_bias_sub_e_kernel(tc, xT, w, b, gate, offs, out):
                 out=codes[:].bitcast(FP8X4), scales=scales[:], in_=grouped[:].rearrange("p n j -> p (n j)")
             )
 
-        def multiply(c):
+        def multiply(c, m):
             grouped, codes, scales = tiles[c]
-            for m in range(MB):
-                rows = slice(m * P, (m + 1) * P)
-                for d in range(D):
-                    cols = slice(d * C, (d + 1) * C)
-                    nc.tensor.matmul_mx(
-                        out=banks[c][m][:],
-                        lhsT=w_codes[d][:, rows].bitcast(FP8X4),
-                        lhsT_scale=w_scales[d][:, rows],
-                        rhs=codes[:, cols].bitcast(FP8X4),
-                        rhs_scale=scales[:, cols],
-                        start=(d == 0),
-                        stop=(d == D - 1),
-                    )
+            for d in range(D):
+                rows = slice(d * P, (d + 1) * P)
+                cols = slice(d * C, (d + 1) * C)
+                nc.tensor.matmul_mx(
+                    out=banks[c][m][:],
+                    lhsT=w_codes[m][:, rows].bitcast(FP8X4),
+                    lhsT_scale=w_scales[m][:, rows],
+                    rhs=codes[:, cols].bitcast(FP8X4),
+                    rhs_scale=scales[:, cols],
+                    start=(d == 0),
+                    stop=(d == D - 1),
+                )
 
         def scatter(c, d, m):
             nc.vector.tensor_tensor(
@@ -118,43 +126,48 @@ def tile_picked_tome_lin_bias_sub_e_kernel(tc, xT, w, b, gate, offs, out):
                         grouped[:, d * C : (d + 1) * C, j], x16[j][:].indirect(entries(c, d)), COPY
                     )
 
-        def cast_w(d):
-            nc.vector.tensor_copy(w16[d][:], w32[d][:].rearrange("p j n -> p n j"))
+        def cast_w(m):
+            nc.vector.tensor_copy(w16[m][:], w32[m][:].rearrange("p d j n -> p d n j"))
 
-        def quantize_w(d):
+        def quantize_w(m):
             nc.vector.quantize_mx(
-                out=w_codes[d][:].bitcast(FP8X4),
-                scales=w_scales[d][:],
-                in_=w16[d][:].rearrange("p n j -> p (n j)"),
+                out=w_codes[m][:].bitcast(FP8X4),
+                scales=w_scales[m][:],
+                in_=w16[m][:].rearrange("p d n j -> p (d n j)"),
             )
 
-        def leave_bank(c):
-            for m in range(MB):
-                nc.scalar.activation(y[c][m][:], banks[c][m][:], IDENT, bias=bias[m][:])
+        def leave_bank_vector(c, m):
+            nc.vector.tensor_scalar(y[c][m][:], banks[c][m][:], bias[m][:], None, ADD)
+
+        def leave_bank(c, m):
+            nc.scalar.activation(y[c][m][:], banks[c][m][:], IDENT, bias=bias[m][:])
 
         cast_w(0)
         quantize_x(0)
-        cast_w(1)
         quantize_w(0)
+        multiply(0, 0)
+        cast_w(1)
+        leave_bank_vector(0, 0)
         quantize_w(1)
-        multiply(0)
-        for m in range(MB):
-            nc.vector.tensor_scalar(y[0][m][:], banks[0][m][:], bias[m][:], None, ADD)
+        multiply(0, 1)
         gather_scalar(1)
         scatter(0, 0, 0)
+        leave_bank_vector(0, 1)
+        scatter(0, 1, 0)
         scatter(0, 0, 1)
         quantize_x(1)
-        multiply(1)
-        leave_bank(1)
-        scatter(0, 1, 0)
+        for m in range(MB):
+            multiply(1, m)
+            leave_bank(1, m)
         scatter(0, 1, 1)
         gather_scalar(2)
         scatter(1, 0, 0)
         scatter(1, 0, 1)
         scatter(1, 1, 0)
         quantize_x(2)
-        multiply(2)
-        leave_bank(2)
+        for m in range(MB):
+            multiply(2, m)
+            leave_bank(2, m)
         scatter(1, 1, 1)
         scatter(2, 0, 0)
         scatter(2, 0, 1)

@@ -20,8 +20,6 @@ P = 128
 PACK = 4
 MB = N // P
 C = 256
-CHUNKS = V // C
-HALF = T // 2
 
 
 def tile_picked_tome_lin_bias_sub_e_kernel(tc, xT, w, b, gate, offs, out):
@@ -33,31 +31,31 @@ def tile_picked_tome_lin_bias_sub_e_kernel(tc, xT, w, b, gate, offs, out):
         lists = keep.tile([P, S // 16], U16, name="lists")
         nc.sync.dma_start(lists[:], offs)
 
-        bias = [keep.tile([P, 1], F32, name=f"bias_{m}") for m in range(MB)]
-        for m in range(MB):
-            nc.scalar.dma_start(bias[m][:], b[m * P : (m + 1) * P, :])
-        x_rows = xT.rearrange("(p j) t -> p j t", j=PACK)
-        x32 = [keep.tile([P, T], F32, name=f"x32_{j}") for j in range(PACK)]
+        x32 = [keep.tile([P, T], F32, name=f"x32_{j}", align_bytes=64) for j in range(PACK)]
         x16 = [keep.tile([P, T], BF16, name=f"x16_{j}") for j in range(PACK)]
-        for j in range(PACK):
-            for h in range(2):
-                cols = slice(h * HALF, (h + 1) * HALF)
-                nc.sync.dma_start(x32[j][:, cols], x_rows[:, j, cols])
+        w32 = [keep.tile([P, PACK, N], F32, name=f"w32_{d}") for d in range(D)]
+        bias = [keep.tile([P, 1], F32, name=f"bias_{m}") for m in range(MB)]
+        gate_a = [keep.tile([P, D, C], F32, name=f"gate_a_{m}") for m in range(MB)]
+        gate_b = [keep.tile([P, D, V - C], F32, name=f"gate_b_{m}") for m in range(MB)]
 
-        w32 = [keep.tile([P, D, PACK, P], F32, name=f"w32_{m}") for m in range(MB)]
-        gates = [[keep.tile([P, D, C], F32, name=f"gate_{c}_{m}") for m in range(MB)] for c in range(CHUNKS)]
+        def load_x(j):
+            nc.sync.dma_start(x32[j][:], xT.rearrange("(p j) t -> p j t", j=PACK)[:, j, :])
 
-        def load_gate(c, m):
-            rows = gate[m * P : (m + 1) * P, :].rearrange("p (d v) -> p d v", d=D)
-            nc.sync.dma_start(gates[c][m][:], rows[:, :, c * C : (c + 1) * C])
-
-        for m in range(MB):
-            for d in range(D):
-                nc.sync.dma_start(w32[m][:, d], w[d].rearrange("(p j) n -> p j n", j=PACK)[:, :, m * P : (m + 1) * P])
-            load_gate(0, m)
-        for c in range(1, CHUNKS):
+        def load_gate(tiles, cols):
             for m in range(MB):
-                load_gate(c, m)
+                rows = gate[m * P : (m + 1) * P, :].rearrange("p (d v) -> p d v", d=D)
+                nc.sync.dma_start(tiles[m][:], rows[:, :, cols])
+
+        load_x(0)
+        load_x(1)
+        load_x(2)
+        for d in range(D):
+            nc.sync.dma_start(w32[d][:], w[d].rearrange("(p j) n -> p j n", j=PACK))
+        load_x(3)
+        for m in range(MB):
+            nc.sync.dma_start(bias[m][:], b[m * P : (m + 1) * P, :])
+        load_gate(gate_a, slice(0, C))
+        load_gate(gate_b, slice(C, V))
 
         window = [keep.tile([P, T], F32, name=f"window_{m}") for m in range(MB)]
         for m in range(MB):
@@ -67,107 +65,102 @@ def tile_picked_tome_lin_bias_sub_e_kernel(tc, xT, w, b, gate, offs, out):
             first = (d * V + c * C) // 16
             return lists[:, first : first + C // 16]
 
-        def chunk_tiles(c):
-            grouped = keep.tile([P, D * C, PACK], BF16, name="grouped", tag="by_vector" if c == 0 else "by_scalar", align_bytes=64)
+        w16 = keep.tile([P, D, N, PACK], BF16, name="w16", align_bytes=64)
+        w_codes = keep.tile([P, D, N], U32, name="w_codes", align_bytes=64)
+        w_scales = keep.tile([P, D, N], U8, name="w_scales", align_bytes=64)
+        y = [[keep.tile([P, C], F32, name=f"y_{c}_{m}") for m in range(MB)] for c in range(3)]
+        banks = [[psum.tile([P, C], F32, name=f"bank_{c}_{m}") for m in range(MB)] for c in range(3)]
+        chunks = {}
+
+        def open_chunk(c, tag):
+            grouped = keep.tile([P, D * C, PACK], BF16, name="grouped", tag=tag, align_bytes=64)
             codes = keep.tile([P, D * C], U32, name="x_codes", tag="x_codes", align_bytes=64)
             scales = keep.tile([P, D * C], U8, name="x_scales", tag="x_scales", align_bytes=64)
-            return grouped, codes, scales
+            chunks[c] = (grouped, codes, scales)
 
-        tiles = {0: chunk_tiles(0)}
-        grouped = tiles[0][0]
-        w16 = [keep.tile([P, D, P, PACK], BF16, name=f"w16_{m}", align_bytes=64) for m in range(MB)]
-        w_codes = [keep.tile([P, D * P], U32, name=f"w_codes_{m}", align_bytes=64) for m in range(MB)]
-        w_scales = [keep.tile([P, D * P], U8, name=f"w_scales_{m}", align_bytes=64) for m in range(MB)]
-        y = [[keep.tile([P, C], F32, name=f"y_{c}_{m}") for m in range(MB)] for c in range(CHUNKS)]
-        banks = [[psum.tile([P, C], F32, name=f"bank_{c}_{m}") for m in range(MB)] for c in range(CHUNKS)]
-
-        for j in range(PACK):
-            for h in range(2):
-                cols = slice(h * HALF, (h + 1) * HALF)
-                if h == 0 or j >= 2:
-                    nc.scalar.activation(x16[j][:, cols], x32[j][:, cols], COPY)
+        def gather_vector(c, j):
+            grouped = chunks[c][0]
             for d in range(D):
-                nc.vector.tensor_copy(grouped[:, d * C : (d + 1) * C, j], x32[j][:].indirect(entries(0, d)))
-            if j < 2:
-                nc.vector.tensor_copy(x16[j][:, HALF:], x32[j][:, HALF:])
+                nc.vector.tensor_copy(grouped[:, d * C : (d + 1) * C, j], x32[j][:].indirect(entries(c, d)))
 
-        def quantize_x(c):
-            grouped, codes, scales = tiles[c]
+        def gather_scalar(c, j):
+            grouped = chunks[c][0]
+            for d in range(D):
+                nc.scalar.activation(grouped[:, d * C : (d + 1) * C, j], x16[j][:].indirect(entries(c, d)), COPY)
+
+        def quantize_x(c, first, last):
+            grouped, codes, scales = chunks[c]
             nc.vector.quantize_mx(
-                out=codes[:].bitcast(FP8X4), scales=scales[:], in_=grouped[:].rearrange("p n j -> p (n j)")
+                out=codes[:, first:last].bitcast(FP8X4),
+                scales=scales[:, first:last],
+                in_=grouped[:, first:last, :].rearrange("p n j -> p (n j)"),
             )
 
         def multiply(c, m):
-            grouped, codes, scales = tiles[c]
+            grouped, codes, scales = chunks[c]
+            rows = slice(m * P, (m + 1) * P)
             for d in range(D):
-                rows = slice(d * P, (d + 1) * P)
                 cols = slice(d * C, (d + 1) * C)
                 nc.tensor.matmul_mx(
                     out=banks[c][m][:],
-                    lhsT=w_codes[m][:, rows].bitcast(FP8X4),
-                    lhsT_scale=w_scales[m][:, rows],
+                    lhsT=w_codes[:, d, rows].bitcast(FP8X4),
+                    lhsT_scale=w_scales[:, d, rows],
                     rhs=codes[:, cols].bitcast(FP8X4),
                     rhs_scale=scales[:, cols],
                     start=(d == 0),
                     stop=(d == D - 1),
                 )
 
-        def scatter(c, d, m):
-            nc.vector.tensor_tensor(
-                window[m][:].indirect(entries(c, d)), y[c][m][:], gates[c][m][:, d, :], MULT
-            )
-
-        def gather_scalar(c):
-            tiles[c] = chunk_tiles(c)
-            grouped = tiles[c][0]
-            for j in range(PACK):
-                for d in range(D):
-                    nc.scalar.activation(
-                        grouped[:, d * C : (d + 1) * C, j], x16[j][:].indirect(entries(c, d)), COPY
-                    )
-
-        def cast_w(m):
-            nc.vector.tensor_copy(w16[m][:], w32[m][:].rearrange("p d j n -> p d n j"))
-
-        def quantize_w(m):
-            nc.vector.quantize_mx(
-                out=w_codes[m][:].bitcast(FP8X4),
-                scales=w_scales[m][:],
-                in_=w16[m][:].rearrange("p d n j -> p (d n j)"),
-            )
-
-        def leave_bank_vector(c, m):
+        def leave_vector(c, m):
             nc.vector.tensor_scalar(y[c][m][:], banks[c][m][:], bias[m][:], None, ADD)
 
-        def leave_bank(c, m):
+        def leave_scalar(c, m):
             nc.scalar.activation(y[c][m][:], banks[c][m][:], IDENT, bias=bias[m][:])
 
-        cast_w(0)
-        quantize_x(0)
-        quantize_w(0)
-        multiply(0, 0)
-        cast_w(1)
-        leave_bank_vector(0, 0)
-        quantize_w(1)
-        multiply(0, 1)
-        gather_scalar(1)
+        def scatter(c, d, m):
+            factor = gate_a[m][:, d, :] if c == 0 else gate_b[m][:, d, (c - 1) * C : c * C]
+            nc.vector.tensor_tensor(window[m][:].indirect(entries(c, d)), y[c][m][:], factor, MULT)
+
+        open_chunk(0, "by_vector")
+        for j in range(PACK):
+            nc.scalar.activation(x16[j][:], x32[j][:], COPY)
+            if j == 3:
+                for d in range(D):
+                    nc.vector.tensor_copy(w16[:, d], w32[d][:].rearrange("p j n -> p n j"))
+                nc.vector.quantize_mx(
+                    out=w_codes[:].rearrange("p d n -> p (d n)").bitcast(FP8X4),
+                    scales=w_scales[:].rearrange("p d n -> p (d n)"),
+                    in_=w16[:].rearrange("p d n j -> p (d n j)"),
+                )
+            gather_vector(0, j)
+        for d in range(D):
+            quantize_x(0, d * C, (d + 1) * C)
+        for m in range(MB):
+            multiply(0, m)
+        for m in range(MB):
+            leave_vector(0, m)
+        open_chunk(1, "by_scalar")
+        for j in range(PACK):
+            gather_scalar(1, j)
         scatter(0, 0, 0)
-        leave_bank_vector(0, 1)
-        scatter(0, 1, 0)
         scatter(0, 0, 1)
-        quantize_x(1)
+        quantize_x(1, 0, D * C)
         for m in range(MB):
             multiply(1, m)
-            leave_bank(1, m)
+        open_chunk(2, "x32_3")
+        for j in range(PACK):
+            gather_scalar(2, j)
+        scatter(0, 1, 0)
         scatter(0, 1, 1)
-        gather_scalar(2)
+        for m in range(MB):
+            leave_vector(1, m)
         scatter(1, 0, 0)
         scatter(1, 0, 1)
         scatter(1, 1, 0)
-        quantize_x(2)
+        quantize_x(2, 0, D * C)
         for m in range(MB):
             multiply(2, m)
-            leave_bank(2, m)
+            leave_scalar(2, m)
         scatter(1, 1, 1)
         scatter(2, 0, 0)
         scatter(2, 0, 1)

from contextlib import ExitStack

import concourse.mybir as mybir

K, T, D, S, V, N = 512, 2048, 2, 1536, 768, 256
FLOPS = 2 * K * D * V * N

F32 = mybir.dt.float32
BF16 = mybir.dt.bfloat16
U32 = mybir.dt.uint32
U16 = mybir.dt.uint16
U8 = mybir.dt.uint8
FP8X4 = mybir.dt.float8_e4m3fn_x4
COPY = mybir.ActivationFunctionType.Copy
IDENT = mybir.ActivationFunctionType.Identity
MULT = mybir.AluOpType.mult
ADD = mybir.AluOpType.add

P = 128
PACK = 4
MB = N // P
C = 256


def tile_picked_tome_lin_bias_sub_e_kernel(tc, xT, w, b, gate, offs, out):
    nc = tc.nc
    with ExitStack() as ctx:
        keep = ctx.enter_context(tc.tile_pool(name="keep", bufs=1))
        psum = ctx.enter_context(tc.psum_pool(name="psum", bufs=1))

        lists = keep.tile([P, S // 16], U16, name="lists")
        nc.sync.dma_start(lists[:], offs)

        x32 = [keep.tile([P, T], F32, name=f"x32_{j}", align_bytes=64) for j in range(PACK)]
        x16 = [keep.tile([P, T], BF16, name=f"x16_{j}") for j in range(PACK)]
        w32 = [keep.tile([P, PACK, N], F32, name=f"w32_{d}") for d in range(D)]
        bias = [keep.tile([P, 1], F32, name=f"bias_{m}") for m in range(MB)]
        gate_a = [keep.tile([P, D, C], F32, name=f"gate_a_{m}") for m in range(MB)]
        gate_b = [keep.tile([P, D, V - C], F32, name=f"gate_b_{m}") for m in range(MB)]

        def load_x(j):
            nc.sync.dma_start(x32[j][:], xT.rearrange("(p j) t -> p j t", j=PACK)[:, j, :])

        def load_gate(tiles, cols):
            for m in range(MB):
                rows = gate[m * P : (m + 1) * P, :].rearrange("p (d v) -> p d v", d=D)
                nc.sync.dma_start(tiles[m][:], rows[:, :, cols])

        load_x(0)
        load_x(1)
        load_x(2)
        for d in range(D):
            nc.sync.dma_start(w32[d][:], w[d].rearrange("(p j) n -> p j n", j=PACK))
        load_x(3)
        for m in range(MB):
            nc.sync.dma_start(bias[m][:], b[m * P : (m + 1) * P, :])
        load_gate(gate_a, slice(0, C))
        load_gate(gate_b, slice(C, V))

        window = [keep.tile([P, T], F32, name=f"window_{m}") for m in range(MB)]
        for m in range(MB):
            nc.gpsimd.memset(window[m][:], 0.0)

        def entries(c, d):
            first = (d * V + c * C) // 16
            return lists[:, first : first + C // 16]

        w16 = keep.tile([P, D, N, PACK], BF16, name="w16", align_bytes=64)
        w_codes = keep.tile([P, D, N], U32, name="w_codes", align_bytes=64)
        w_scales = keep.tile([P, D, N], U8, name="w_scales", align_bytes=64)
        y = [[keep.tile([P, C], F32, name=f"y_{c}_{m}") for m in range(MB)] for c in range(3)]
        banks = [[psum.tile([P, C], F32, name=f"bank_{c}_{m}") for m in range(MB)] for c in range(3)]
        chunks = {}

        def open_chunk(c, tag):
            grouped = keep.tile([P, D * C, PACK], BF16, name="grouped", tag=tag, align_bytes=64)
            codes = keep.tile([P, D * C], U32, name="x_codes", tag="x_codes", align_bytes=64)
            scales = keep.tile([P, D * C], U8, name="x_scales", tag="x_scales", align_bytes=64)
            chunks[c] = (grouped, codes, scales)

        def gather_vector(c, j):
            grouped = chunks[c][0]
            for d in range(D):
                nc.vector.tensor_copy(grouped[:, d * C : (d + 1) * C, j], x32[j][:].indirect(entries(c, d)))

        def gather_scalar(c, j):
            grouped = chunks[c][0]
            for d in range(D):
                nc.scalar.activation(grouped[:, d * C : (d + 1) * C, j], x16[j][:].indirect(entries(c, d)), COPY)

        def quantize_x(c, first, last):
            grouped, codes, scales = chunks[c]
            nc.vector.quantize_mx(
                out=codes[:, first:last].bitcast(FP8X4),
                scales=scales[:, first:last],
                in_=grouped[:, first:last, :].rearrange("p n j -> p (n j)"),
            )

        def multiply(c, m):
            grouped, codes, scales = chunks[c]
            rows = slice(m * P, (m + 1) * P)
            for d in range(D):
                cols = slice(d * C, (d + 1) * C)
                nc.tensor.matmul_mx(
                    out=banks[c][m][:],
                    lhsT=w_codes[:, d, rows].bitcast(FP8X4),
                    lhsT_scale=w_scales[:, d, rows],
                    rhs=codes[:, cols].bitcast(FP8X4),
                    rhs_scale=scales[:, cols],
                    start=(d == 0),
                    stop=(d == D - 1),
                )

        def leave_vector(c, m):
            nc.vector.tensor_scalar(y[c][m][:], banks[c][m][:], bias[m][:], None, ADD)

        def leave_scalar(c, m):
            nc.scalar.activation(y[c][m][:], banks[c][m][:], IDENT, bias=bias[m][:])

        def scatter(c, d, m):
            factor = gate_a[m][:, d, :] if c == 0 else gate_b[m][:, d, (c - 1) * C : c * C]
            nc.vector.tensor_tensor(window[m][:].indirect(entries(c, d)), y[c][m][:], factor, MULT)

        open_chunk(0, "by_vector")
        for j in range(PACK):
            nc.scalar.activation(x16[j][:], x32[j][:], COPY)
            if j == 3:
                for d in range(D):
                    nc.vector.tensor_copy(w16[:, d], w32[d][:].rearrange("p j n -> p n j"))
                nc.vector.quantize_mx(
                    out=w_codes[:].rearrange("p d n -> p (d n)").bitcast(FP8X4),
                    scales=w_scales[:].rearrange("p d n -> p (d n)"),
                    in_=w16[:].rearrange("p d n j -> p (d n j)"),
                )
            gather_vector(0, j)
        for d in range(D):
            quantize_x(0, d * C, (d + 1) * C)
        for m in range(MB):
            multiply(0, m)
        for m in range(MB):
            leave_vector(0, m)
        open_chunk(1, "by_scalar")
        for j in range(PACK):
            gather_scalar(1, j)
        scatter(0, 0, 0)
        scatter(0, 0, 1)
        quantize_x(1, 0, D * C)
        for m in range(MB):
            multiply(1, m)
        open_chunk(2, "x32_3")
        for j in range(PACK):
            gather_scalar(2, j)
        scatter(0, 1, 0)
        scatter(0, 1, 1)
        for m in range(MB):
            leave_vector(1, m)
        scatter(1, 0, 0)
        scatter(1, 0, 1)
        scatter(1, 1, 0)
        quantize_x(2, 0, D * C)
        for m in range(MB):
            multiply(2, m)
            leave_scalar(2, m)
        scatter(1, 1, 1)
        scatter(2, 0, 0)
        scatter(2, 0, 1)
        scatter(2, 1, 0)
        nc.sync.dma_start(out[0:P, :], window[0][:])
        scatter(2, 1, 1)
        nc.sync.dma_start(out[P:, :], window[1][:])
